import numpy as np
import ml_dtypes


def mxq(x, axis, fmt="e4m3"):
    dtype, down = {"e4m3": (ml_dtypes.float8_e4m3fn, 7), "e5m2": (ml_dtypes.float8_e5m2, 14)}[fmt]
    v = np.moveaxis(np.asarray(x, np.float32).astype(ml_dtypes.bfloat16).astype(np.float64), axis, -1)
    blocks = v.reshape(v.shape[:-1] + (-1, 32))
    amax = np.abs(blocks).max(-1, keepdims=True)
    byte = np.maximum(np.where(amax > 0, np.frexp(amax)[1] - 1 + 127, 0) - down, 1)
    scale = np.exp2(byte - 127.0)
    codes = (blocks / scale).astype(np.float32).astype(dtype).astype(np.float64)
    return np.moveaxis((codes * scale).reshape(v.shape), -1, axis)


WIDE = False


def mx_kscale(k):
    if not WIDE:
        return np.ones(k)
    levels = np.array([10, -10, 5, -5, 0])
    if k % 512:
        return np.exp2(np.random.permutation(np.resize(levels, k // 32))).repeat(32)
    a = np.empty((k // 512, 16))
    for p in range(k // 512):
        a[p, :8] = np.random.permutation(np.resize(levels, 8))
        for g in range(8):
            far = levels[np.abs(levels - a[p, g]) >= 10]
            a[p, g + 8] = far[np.random.randint(len(far))]
    return np.exp2(a.ravel()).repeat(32)


def f64(x):
    return np.asarray(x).astype(np.float64)


def striped(idx):
    return np.tile(np.asarray(idx).reshape(-1, 16).T, (8, 1)).astype(np.uint16)


def unstriped(offs):
    return offs[:16].T.reshape(-1).astype(np.int64)


def striped8(idx):
    return np.asarray(idx).reshape(8, -1, 16).transpose(0, 2, 1).reshape(128, -1).astype(np.uint16)


def unstriped8(offs):
    return offs.reshape(8, 16, -1).transpose(0, 2, 1).reshape(8, -1).astype(np.int64)


def pick8(x, idx, run):
    r = np.arange(len(x))
    return x[r[:, None], idx[r % (8 * run) // run]]


E2M1 = np.array([0.0, 0.5, 1.0, 1.5, 2.0, 3.0, 4.0, 6.0, -0.0, -0.5, -1.0, -1.5, -2.0, -3.0, -4.0, -6.0])


def pack_weight(w, fmt):
    k, n = w.shape
    w = f64(np.asarray(w, np.float32).astype(ml_dtypes.bfloat16)).reshape(k // 32, 32, n)
    amax = np.abs(w).max(1)
    if fmt == "e4m3":
        byte = np.frexp(amax)[1] - 1 + 127 - 7
    else:
        mant, ex = np.frexp(amax / 6.0)
        byte = np.where(mant > 0.5, ex, ex - 1) + 127
    byte = np.clip(np.where(amax > 0, byte, 1), 1, 254)
    scaled = (w * np.exp2(127.0 - byte)[:, None, :]).reshape(k, n).astype(np.float32)
    by_word = np.ascontiguousarray(scaled.reshape(k // 512, 128, 4, n).transpose(0, 1, 3, 2))
    if fmt == "e4m3":
        words = by_word.astype(ml_dtypes.float8_e4m3fn).view(np.uint8)
    else:
        c = by_word.astype(ml_dtypes.float4_e2m1fn).view(np.uint8) & 0xF
        words = (c[..., 0::2] | (c[..., 1::2] << 4)).reshape(k // 512, 128, 2 * n)
    return np.ascontiguousarray(words), np.ascontiguousarray(byte.astype(np.uint8).reshape(k // 512, 16, n))


def unpack_weight(words, scales, fmt):
    g, _, n = scales.shape
    words = np.ascontiguousarray(words).reshape(g, 128, n, -1)
    if fmt == "e4m3":
        vals = words.view(ml_dtypes.float8_e4m3fn).astype(np.float64)
    else:
        nib = np.empty((g, 128, n, 4), np.uint8)
        nib[..., 0::2] = words & 0xF
        nib[..., 1::2] = words >> 4
        vals = E2M1[nib]
    vals = vals * np.repeat(np.exp2(scales.astype(np.float64) - 127.0), 8, axis=1)[..., None]
    return vals.transpose(0, 1, 3, 2).reshape(g * 512, n)


K, R, F, T, J, U = 512, 128, 512, 2048, 512, 1024


def setup_inputs():
    n = np.random.standard_normal
    idx = np.random.permutation(T)[:J]
    idx2 = np.stack([np.random.permutation(U)[:J] for _ in range(8)])
    idx3 = np.stack([np.random.permutation(U)[:J] for _ in range(8)])
    fk = mx_kscale(K)
    ff = mx_kscale(F)
    tabp = pack_weight(n((K, T)) / fk[:, None], "e2m1")
    return {
        "tab_words": tabp[0],
        "tab_scales": tabp[1],
        "w1": (n((K, R)) * 1 / np.sqrt(K) * fk[:, None]).astype(np.float32),
        "gain": (np.random.uniform(0.5, 1.5, (R, 1))).astype(np.float32),
        "ground": (n((R, U)) * 0.7).astype(np.float32),
        "wo": (n((F, R)) * 1 / np.sqrt(F) * ff[:, None]).astype(np.float32),
        "dy": (n((F, U)) / ff[:, None]).astype(np.float32),
        "old": (0.5 * n((R, J))).astype(np.float32),
        "offs": striped(idx),
        "offs2": striped8(idx2),
        "offs3": striped8(idx3),
    }


def reference(tab_words, tab_scales, w1, gain, ground, wo, dy, old, offs, offs2, offs3):
    idx = unstriped(offs)
    idx2 = unstriped8(offs2)
    idx3 = unstriped8(offs3)
    tabu = unpack_weight(tab_words, tab_scales, "e2m1")
    w1q = mxq(f64(w1), 0, "e4m3")
    tabidxg = tabu[:, idx]
    a = w1q.T @ tabidxg
    h0 = np.tanh(a)
    h1 = h0 * f64(gain)
    pa = np.zeros((R, U))
    pa[np.arange(R)[:, None], idx2[np.arange(R) % 128 // 16]] = h1
    pb = np.zeros((R, U))
    pb[np.arange(R)[:, None], idx3[np.arange(R) % 128 // 16]] = a
    woq = mxq(f64(wo), 0, "e4m3")
    dyq = mxq(f64(dy), 0, "e4m3")
    c0 = woq.T @ dyq
    dpb = c0 * (pa + f64(ground)) / np.square(np.square(pb) + 1.0) * (-1.0) * pb * 2.0
    dpa = c0 / (np.square(pb) + 1.0)
    dh1 = pick8(dpa, idx2, 16)
    dh0 = dh1 * f64(gain)
    da = pick8(dpb, idx3, 16) + dh0 * (1.0 - np.square(h0))
    y = da + f64(old)
    return y

@@ -1,0 +1,163 @@
+from contextlib import ExitStack
+
+import concourse.mybir as mybir
+
+K, R, F, T, J, U = 512, 128, 512, 2048, 512, 1024
+FLOPS = 2 * K * R * J + 2 * F * R * U
+
+F32 = mybir.dt.float32
+BF16 = mybir.dt.bfloat16
+I32 = mybir.dt.int32
+U32 = mybir.dt.uint32
+U16 = mybir.dt.uint16
+U8 = mybir.dt.uint8
+FP8X4 = mybir.dt.float8_e4m3fn_x4
+FP4X4 = mybir.dt.float4_e2m1fn_x4
+ACT = mybir.ActivationFunctionType
+ALU = mybir.AluOpType
+
+P = 128
+PACK = 4
+JH = J // 2
+UH = U // 2
+DY_CHUNK = 256
+
+
+def woven(grouped, raw):
+    return (
+        grouped[:].rearrange("p (c i) t -> p c t i", i=4),
+        raw[:].rearrange("p t (c i) -> p c t i", i=4),
+    )
+
+
+def tile_attend_cpageratio_kernel(tc, tab_words, tab_scales, w1, gain, ground, wo, dy, old, offs, offs2, offs3, out):
+    nc = tc.nc
+    with ExitStack() as ctx:
+        sb = ctx.enter_context(tc.tile_pool(name="sb", bufs=1))
+        ps = ctx.enter_context(tc.psum_pool(name="ps", bufs=1))
+
+        list_tab = sb.tile([P, J // 16], U16, name="list_tab")
+        list_a = sb.tile([P, J // 16], U16, name="list_a")
+        list_b = sb.tile([P, J // 16], U16, name="list_b")
+        words = sb.tile([P, T], U16, name="words")
+        bytes_all = sb.tile([P, T], U8, name="bytes_all")
+        w1_raw = sb.tile([P, PACK, R], F32, name="w1_raw")
+        wo_raw = sb.tile([P, PACK, R], F32, name="wo_raw")
+        n_chunks = U // DY_CHUNK
+        dy_raw = [sb.tile([P, PACK, DY_CHUNK], F32, name="dy_raw%d" % c) for c in range(n_chunks)]
+        gain_sb = sb.tile([P, 1], F32, name="gain_sb")
+        ground_sb = sb.tile([P, U], F32, name="ground_sb")
+        old_sb = sb.tile([P, J], F32, name="old_sb")
+        page_a = sb.tile([P, U], F32, name="page_a")
+        page_b = sb.tile([P, U], F32, name="page_b")
+        warm = sb.tile([P, 1], F32, name="warm")
+        warm_out = sb.tile([P, 1], F32, name="warm_out")
+
+        nc.vector.memset(bytes_all[:].bitcast(I32), 0)
+        nc.vector.memset(warm[:], 0.0)
+        nc.scalar.activation(warm_out[:], warm[:], ACT.Tanh)
+        nc.vector.memset(page_b[:], 0.0)
+        nc.vector.memset(page_a[:], 0.0)
+
+        dy_rows = dy.rearrange("(p t) u -> p t u", t=PACK)
+        nc.sync.dma_start(list_tab[:], offs)
+        nc.sync.dma_start(w1_raw[:], w1.rearrange("(p t) r -> p t r", t=PACK))
+        for q in range(4):
+            nc.sync.dma_start(bytes_all[32 * q : 32 * q + 4, :].bitcast(I32), tab_scales[0, 4 * q : 4 * q + 4, :].bitcast(I32))
+        nc.sync.dma_start(words[:].bitcast(I32), tab_words[0].bitcast(I32))
+        nc.sync.dma_start(dy_raw[0][:], dy_rows[:, :, 0:DY_CHUNK])
+        nc.sync.dma_start(wo_raw[:], wo.rearrange("(p t) r -> p t r", t=PACK))
+        nc.sync.dma_start(list_b[:], offs3)
+        nc.sync.dma_start(list_a[:], offs2)
+        nc.sync.dma_start(gain_sb[:], gain)
+        for c in range(1, n_chunks):
+            nc.sync.dma_start(dy_raw[c][:], dy_rows[:, :, c * DY_CHUNK : (c + 1) * DY_CHUNK])
+        nc.sync.dma_start(ground_sb[:], ground)
+        nc.sync.dma_start(old_sb[:], old)
+
+        w1_g = sb.tile([P, R, PACK], BF16, name="w1_g", align_bytes=64)
+        wo_g = sb.tile([P, R, PACK], BF16, name="wo_g", align_bytes=64)
+        w1_codes = sb.tile([P, R], U32, name="w1_codes", align_bytes=64)
+        w1_sc = sb.tile([P, R], U8, name="w1_sc", align_bytes=64)
+        wo_codes = sb.tile([P, R], U32, name="wo_codes", align_bytes=64)
+        wo_sc = sb.tile([P, R], U8, name="wo_sc", align_bytes=64)
+        nc.scalar.copy(*woven(w1_g, w1_raw))
+
+        tab_sc = sb.tile([P, J], U8, name="tab_sc", align_bytes=64)
+        nc.vector.tensor_copy(tab_sc[:], bytes_all[:].indirect(list_tab[:]))
+        nc.vector.quantize_mx(w1_codes[:].bitcast(FP8X4), w1_sc[:], w1_g[:].rearrange("p c t -> p (c t)"))
+
+
+        a_sb = sb.tile([P, J], F32, name="a_sb")
+        h0 = sb.tile([P, J], F32, name="h0")
+        halves = [slice(h * JH, (h + 1) * JH) for h in range(2)]
+        cols = [slice(h * JH // 16, (h + 1) * JH // 16) for h in range(2)]
+        a_ps = [ps.tile([P, JH], F32, name="a_ps%d" % h) for h in range(2)]
+        for h in range(2):
+            tab_w = sb.tile([P, JH], U16, name="tab_w%d" % h, align_bytes=64)
+            nc.vector.tensor_copy(tab_w[:], words[:].indirect(list_tab[:, cols[h]]))
+            nc.tensor.matmul_mx(a_ps[h][:], lhsT=w1_codes[:].bitcast(FP8X4), lhsT_scale=w1_sc[:],
+                                rhs=tab_w[:].bitcast(FP4X4), rhs_scale=tab_sc[:, halves[h]], start=True, stop=True)
+            nc.scalar.copy(a_sb[:, halves[h]], a_ps[h][:])
+
+        dy_g = [sb.tile([P, DY_CHUNK, PACK], BF16, name="dy_g%d" % c, align_bytes=64) for c in range(n_chunks)]
+        dy_codes = sb.tile([P, U], U32, name="dy_codes", align_bytes=64)
+        dy_sc = sb.tile([P, U], U8, name="dy_sc", align_bytes=64)
+
+        def quantise_dy(c):
+            cs = slice(c * DY_CHUNK, (c + 1) * DY_CHUNK)
+            nc.vector.quantize_mx(dy_codes[:, cs].bitcast(FP8X4), dy_sc[:, cs], dy_g[c][:].rearrange("p c t -> p (c t)"))
+
+        nc.vector.tensor_copy(*woven(dy_g[0], dy_raw[0]))
+        for h in range(2):
+            nc.vector.tensor_copy(page_b[:].indirect(list_b[:, cols[h]]), a_sb[:, halves[h]])
+        for h in range(2):
+            nc.scalar.activation(h0[:, halves[h]], a_ps[h][:], ACT.Tanh)
+        gain_wide = sb.tile([P, J], F32, name="gain_wide")
+        nc.scalar.copy(gain_wide[:], gain_sb[:, 0:1].to_broadcast([P, J]))
+        nc.scalar.copy(*woven(wo_g, wo_raw))
+        for c in range(1, n_chunks):
+            nc.scalar.copy(*woven(dy_g[c], dy_raw[c]))
+        nc.vector.tensor_tensor(page_a[:].indirect(list_a[:]), h0[:], gain_wide[:], ALU.mult)
+
+        nc.vector.quantize_mx(wo_codes[:].bitcast(FP8X4), wo_sc[:], wo_g[:].rearrange("p c t -> p (c t)"))
+        for c in range(n_chunks):
+            quantise_dy(c)
+
+        us = [slice(h * UH, (h + 1) * UH) for h in range(2)]
+        c0 = [ps.tile([P, UH], F32, name="c0_%d" % h) for h in range(2)]
+        for h in range(2):
+            nc.tensor.matmul_mx(c0[h][:], lhsT=wo_codes[:].bitcast(FP8X4), lhsT_scale=wo_sc[:],
+                                rhs=dy_codes[:, us[h]].bitcast(FP8X4), rhs_scale=dy_sc[:, us[h]], start=True, stop=True)
+
+        sq = dy_raw[n_chunks - 1][:].rearrange("p t c -> p (t c)")
+        rs = sb.tile([P, U], F32, name="rs")
+        rec = sb.tile([P, U], F32, name="rec")
+        for h in range(2):
+            nc.scalar.activation(sq[:, us[h]], page_b[:, us[h]], ACT.Square)
+            nc.scalar.activation(rs[:, us[h]], sq[:, us[h]], ACT.Abs_reciprocal_sqrt, bias=1.0)
+            nc.scalar.activation(rec[:, us[h]], rs[:, us[h]], ACT.Square)
+        h0_sq = sb.tile([P, J], F32, name="h0_sq")
+        slope = sb.tile([P, J], F32, name="slope")
+        nc.scalar.activation(h0_sq[:], h0[:], ACT.Square)
+        nc.scalar.activation(slope[:], h0_sq[:], ACT.Copy, bias=1.0, scale=-1.0)
+
+        top = sb.tile([P, U], F32, name="top")
+        nc.vector.tensor_tensor(top[:], page_a[:], ground_sb[:], ALU.add)
+        top_b = sb.tile([P, U], F32, name="top_b")
+        nc.vector.scalar_tensor_tensor(top_b[:], page_b[:], -2.0, top[:], ALU.mult, ALU.mult)
+        dpa = sb.tile([P, U], F32, name="dpa")
+        dpb = sb.tile([P, U], F32, name="dpb")
+        part = sb.tile([P, U], F32, name="part")
+        for h in range(2):
+            nc.vector.tensor_tensor(dpa[:, us[h]], c0[h][:], rec[:, us[h]], ALU.mult)
+            nc.vector.tensor_tensor(part[:, us[h]], top_b[:, us[h]], rec[:, us[h]], ALU.mult)
+        dz = sb.tile([P, J], F32, name="dz")
+        nc.vector.tensor_tensor(dpb[:], part[:], dpa[:], ALU.mult)
+        nc.vector.tensor_tensor(dz[:], dpa[:].indirect(list_a[:]), slope[:], ALU.mult)
+        rest = sb.tile([P, J], F32, name="rest")
+        nc.vector.scalar_tensor_tensor(rest[:], dz[:], gain_sb[:, 0:1], old_sb[:], ALU.mult, ALU.add)
+        for h in range(2):
+            res = sb.tile([P, JH], F32, name="res%d" % h)
+            nc.vector.tensor_tensor(res[:], dpb[:].indirect(list_b[:, cols[h]]), rest[:, halves[h]], ALU.add)
+            nc.sync.dma_start(out[:, halves[h]], res[:])

@@ -1,6 +1,7 @@
 from contextlib import ExitStack
 
 import concourse.mybir as mybir
+from concourse.masks import make_identity
 
 K, R, F, T, J, U = 512, 128, 512, 2048, 512, 1024
 FLOPS = 2 * K * R * J + 2 * F * R * U
@@ -46,7 +47,7 @@ def tile_attend_cpageratio_kernel(tc, tab_words, tab_scales, w1, gain, ground, w
         n_chunks = U // DY_CHUNK
         dy_raw = [sb.tile([P, PACK, DY_CHUNK], F32, name="dy_raw%d" % c) for c in range(n_chunks)]
         gain_sb = sb.tile([P, 1], F32, name="gain_sb")
-        ground_sb = sb.tile([P, U], F32, name="ground_sb")
+        ground_sb = sb.tile([P, U], F32, name="ground_sb", tag="ground_then_codes", align_bytes=64)
         old_sb = sb.tile([P, J], F32, name="old_sb")
         page_a = sb.tile([P, U], F32, name="page_a")
         page_b = sb.tile([P, U], F32, name="page_b")
@@ -59,17 +60,19 @@ def tile_attend_cpageratio_kernel(tc, tab_words, tab_scales, w1, gain, ground, w
         nc.vector.memset(page_b[:], 0.0)
         nc.vector.memset(page_a[:], 0.0)
 
+        ident = sb.tile([P, P], F32, name="ident")
+        make_identity(nc, ident[:])
         dy_rows = dy.rearrange("(p t) u -> p t u", t=PACK)
         nc.sync.dma_start(list_tab[:], offs)
         nc.sync.dma_start(w1_raw[:], w1.rearrange("(p t) r -> p t r", t=PACK))
         for q in range(4):
             nc.sync.dma_start(bytes_all[32 * q : 32 * q + 4, :].bitcast(I32), tab_scales[0, 4 * q : 4 * q + 4, :].bitcast(I32))
         nc.sync.dma_start(words[:].bitcast(I32), tab_words[0].bitcast(I32))
-        nc.sync.dma_start(dy_raw[0][:], dy_rows[:, :, 0:DY_CHUNK])
         nc.sync.dma_start(wo_raw[:], wo.rearrange("(p t) r -> p t r", t=PACK))
-        nc.sync.dma_start(list_b[:], offs3)
-        nc.sync.dma_start(list_a[:], offs2)
         nc.sync.dma_start(gain_sb[:], gain)
+        nc.sync.dma_start(list_b[:], offs3)
+        nc.sync.dma_start(dy_raw[0][:], dy_rows[:, :, 0:DY_CHUNK])
+        nc.sync.dma_start(list_a[:], offs2)
         for c in range(1, n_chunks):
             nc.sync.dma_start(dy_raw[c][:], dy_rows[:, :, c * DY_CHUNK : (c + 1) * DY_CHUNK])
         nc.sync.dma_start(ground_sb[:], ground)
@@ -101,28 +104,36 @@ def tile_attend_cpageratio_kernel(tc, tab_words, tab_scales, w1, gain, ground, w
             nc.scalar.copy(a_sb[:, halves[h]], a_ps[h][:])
 
         dy_g = [sb.tile([P, DY_CHUNK, PACK], BF16, name="dy_g%d" % c, align_bytes=64) for c in range(n_chunks)]
-        dy_codes = sb.tile([P, U], U32, name="dy_codes", align_bytes=64)
         dy_sc = sb.tile([P, U], U8, name="dy_sc", align_bytes=64)
 
-        def quantise_dy(c):
-            cs = slice(c * DY_CHUNK, (c + 1) * DY_CHUNK)
-            nc.vector.quantize_mx(dy_codes[:, cs].bitcast(FP8X4), dy_sc[:, cs], dy_g[c][:].rearrange("p c t -> p (c t)"))
-
-        nc.vector.tensor_copy(*woven(dy_g[0], dy_raw[0]))
+        nc.vector.tensor_copy(*woven(wo_g, wo_raw))
+        nc.vector.quantize_mx(wo_codes[:].bitcast(FP8X4), wo_sc[:], wo_g[:].rearrange("p c t -> p (c t)"))
         for h in range(2):
             nc.vector.tensor_copy(page_b[:].indirect(list_b[:, cols[h]]), a_sb[:, halves[h]])
         for h in range(2):
             nc.scalar.activation(h0[:, halves[h]], a_ps[h][:], ACT.Tanh)
-        gain_wide = sb.tile([P, J], F32, name="gain_wide")
-        nc.scalar.copy(gain_wide[:], gain_sb[:, 0:1].to_broadcast([P, J]))
-        nc.scalar.copy(*woven(wo_g, wo_raw))
+        neg_gain = sb.tile([P, 1], F32, name="neg_gain")
+        nc.gpsimd.tensor_scalar(neg_gain[:], gain_sb[:], -1.0, 0.0, ALU.mult, ALU.add)
+        h1 = sb.tile([P, J], F32, name="h1")
+        nc.gpsimd.tensor_scalar(h1[:], h0[:], gain_sb[:, 0:1], 1.0, ALU.mult, ALU.mult)
+        nc.scalar.copy(*woven(dy_g[0], dy_raw[0]))
+        warm_root = sb.tile([P, 1], F32, name="warm_root")
+        nc.scalar.activation(warm_root[:], h0[:, J - 1 : J], ACT.Abs_reciprocal_sqrt, bias=1.0, scale=0.0)
         for c in range(1, n_chunks):
-            nc.scalar.copy(*woven(dy_g[c], dy_raw[c]))
-        nc.vector.tensor_tensor(page_a[:].indirect(list_a[:]), h0[:], gain_wide[:], ALU.mult)
-
-        nc.vector.quantize_mx(wo_codes[:].bitcast(FP8X4), wo_sc[:], wo_g[:].rearrange("p c t -> p (c t)"))
+            nc.gpsimd.tensor_scalar(dy_g[c][:], dy_raw[c][:].rearrange("p t c -> p c t"), 1.0, 0.0, ALU.mult, ALU.add)
+        nc.vector.tensor_copy(page_a[:].indirect(list_a[:]), h1[:])
+        top_t = [ps.tile([P, UH], F32, name="top_t%d" % h) for h in range(2)]
+        top = [ps.tile([P, UH], F32, name="top%d" % h) for h in range(2)]
+        top_sb = sb.tile([P, U], F32, name="top_sb")
+        blocks = UH // P
+        for h in range(2):
+            for b in range(blocks):
+                nc.tensor.matmul(top_t[h][:, b * P : (b + 1) * P], lhsT=ground_sb[:, h * UH + b * P : h * UH + (b + 1) * P],
+                                 rhs=ident[:], is_transpose=True, start=(b == 0), stop=False)
+        dy_codes = sb.tile([P, U], U32, name="dy_codes", tag="ground_then_codes", align_bytes=64)
         for c in range(n_chunks):
-            quantise_dy(c)
+            cs = slice(c * DY_CHUNK, (c + 1) * DY_CHUNK)
+            nc.vector.quantize_mx(dy_codes[:, cs].bitcast(FP8X4), dy_sc[:, cs], dy_g[c][:].rearrange("p c t -> p (c t)"))
 
         us = [slice(h * UH, (h + 1) * UH) for h in range(2)]
         c0 = [ps.tile([P, UH], F32, name="c0_%d" % h) for h in range(2)]
@@ -130,33 +141,52 @@ def tile_attend_cpageratio_kernel(tc, tab_words, tab_scales, w1, gain, ground, w
             nc.tensor.matmul_mx(c0[h][:], lhsT=wo_codes[:].bitcast(FP8X4), lhsT_scale=wo_sc[:],
                                 rhs=dy_codes[:, us[h]].bitcast(FP8X4), rhs_scale=dy_sc[:, us[h]], start=True, stop=True)
 
-        sq = dy_raw[n_chunks - 1][:].rearrange("p t c -> p (t c)")
+        sq = dy_raw[0][:].rearrange("p t c -> p (t c)")
         rs = sb.tile([P, U], F32, name="rs")
         rec = sb.tile([P, U], F32, name="rec")
         for h in range(2):
-            nc.scalar.activation(sq[:, us[h]], page_b[:, us[h]], ACT.Square)
-            nc.scalar.activation(rs[:, us[h]], sq[:, us[h]], ACT.Abs_reciprocal_sqrt, bias=1.0)
-            nc.scalar.activation(rec[:, us[h]], rs[:, us[h]], ACT.Square)
-        h0_sq = sb.tile([P, J], F32, name="h0_sq")
+            quarters = [slice(h * UH + e * UH // 2, h * UH + (e + 1) * UH // 2) for e in range(2)]
+            for s in quarters:
+                nc.scalar.activation(sq[:, s], page_b[:, s], ACT.Square)
+            for s in quarters:
+                nc.scalar.activation(rs[:, s], sq[:, s], ACT.Abs_reciprocal_sqrt, bias=1.0)
+            for s in quarters:
+                nc.scalar.activation(rec[:, s], rs[:, s], ACT.Square)
+        h0_sq = rs[:, us[1]]
         slope = sb.tile([P, J], F32, name="slope")
-        nc.scalar.activation(h0_sq[:], h0[:], ACT.Square)
-        nc.scalar.activation(slope[:], h0_sq[:], ACT.Copy, bias=1.0, scale=-1.0)
+        for h in range(2):
+            nc.scalar.activation(h0_sq[:, halves[h]], h0[:, halves[h]], ACT.Square)
+        for h in range(2):
+            nc.scalar.activation(slope[:, halves[h]], h0_sq[:, halves[h]], ACT.Identity, bias=gain_sb[:, 0:1], scale=neg_gain[:, 0:1])
 
-        top = sb.tile([P, U], F32, name="top")
-        nc.vector.tensor_tensor(top[:], page_a[:], ground_sb[:], ALU.add)
-        top_b = sb.tile([P, U], F32, name="top_b")
-        nc.vector.scalar_tensor_tensor(top_b[:], page_b[:], -2.0, top[:], ALU.mult, ALU.mult)
+        bend = [
+            dy_raw[n_chunks - 1][:].rearrange("p t c -> p (t c)")[:, 0:UH],
+            dy_g[n_chunks - 1][:].rearrange("p c t -> p (c t)").bitcast(F32),
+        ]
+        for h in range(2):
+            nc.gpsimd.tensor_tensor(bend[h], page_b[:, us[h]], rec[:, us[h]], ALU.mult)
+
+        for h in range(2):
+            for b in range(blocks):
+                nc.tensor.matmul(top_t[h][:, b * P : (b + 1) * P], lhsT=page_a[:, h * UH + b * P : h * UH + (b + 1) * P],
+                                 rhs=ident[:], is_transpose=True, start=False, stop=(b == blocks - 1))
+            nc.scalar.copy(top_sb[:, us[h]], top_t[h][:])
+        for h in range(2):
+            for b in range(UH // P):
+                nc.tensor.transpose(top[h][:, b * P : (b + 1) * P], top_sb[:, h * UH + b * P : h * UH + (b + 1) * P], ident[:])
+
         dpa = sb.tile([P, U], F32, name="dpa")
         dpb = sb.tile([P, U], F32, name="dpb")
         part = sb.tile([P, U], F32, name="part")
         for h in range(2):
             nc.vector.tensor_tensor(dpa[:, us[h]], c0[h][:], rec[:, us[h]], ALU.mult)
-            nc.vector.tensor_tensor(part[:, us[h]], top_b[:, us[h]], rec[:, us[h]], ALU.mult)
         dz = sb.tile([P, J], F32, name="dz")
-        nc.vector.tensor_tensor(dpb[:], part[:], dpa[:], ALU.mult)
         nc.vector.tensor_tensor(dz[:], dpa[:].indirect(list_a[:]), slope[:], ALU.mult)
         rest = sb.tile([P, J], F32, name="rest")
-        nc.vector.scalar_tensor_tensor(rest[:], dz[:], gain_sb[:, 0:1], old_sb[:], ALU.mult, ALU.add)
+        nc.gpsimd.tensor_tensor(rest[:], dz[:], old_sb[:], ALU.add)
+        for h in range(2):
+            nc.vector.scalar_tensor_tensor(part[:, us[h]], top[h][:], -2.0, bend[h], ALU.mult, ALU.mult)
+        nc.vector.tensor_tensor(dpb[:], part[:], dpa[:], ALU.mult)
         for h in range(2):
             res = sb.tile([P, JH], F32, name="res%d" % h)
             nc.vector.tensor_tensor(res[:], dpb[:].indirect(list_b[:, cols[h]]), rest[:, halves[h]], ALU.add)

@@ -27,7 +27,7 @@ DY_CHUNK = 256
 def woven(grouped, raw):
     return (
         grouped[:].rearrange("p (c i) t -> p c t i", i=4),
-        raw[:].rearrange("p t (c i) -> p c t i", i=4),
+        raw.rearrange("p t (c i) -> p c t i", i=4),
     )
 
 
@@ -45,7 +45,9 @@ def tile_attend_cpageratio_kernel(tc, tab_words, tab_scales, w1, gain, ground, w
         w1_raw = sb.tile([P, PACK, R], F32, name="w1_raw")
         wo_raw = sb.tile([P, PACK, R], F32, name="wo_raw")
         n_chunks = U // DY_CHUNK
-        dy_raw = [sb.tile([P, PACK, DY_CHUNK], F32, name="dy_raw%d" % c) for c in range(n_chunks)]
+        dy_first = sb.tile([P, PACK, 2 * DY_CHUNK], F32, name="dy_first")
+        dy_late = [sb.tile([P, PACK, DY_CHUNK], F32, name="dy_late%d" % c) for c in range(2)]
+        dy_raw = [dy_first[:, :, 0:DY_CHUNK], dy_first[:, :, DY_CHUNK : 2 * DY_CHUNK], dy_late[0][:], dy_late[1][:]]
         gain_sb = sb.tile([P, 1], F32, name="gain_sb")
         ground_sb = sb.tile([P, U], F32, name="ground_sb", tag="ground_then_codes", align_bytes=64)
         old_sb = sb.tile([P, J], F32, name="old_sb")
@@ -71,10 +73,10 @@ def tile_attend_cpageratio_kernel(tc, tab_words, tab_scales, w1, gain, ground, w
         nc.sync.dma_start(wo_raw[:], wo.rearrange("(p t) r -> p t r", t=PACK))
         nc.sync.dma_start(gain_sb[:], gain)
         nc.sync.dma_start(list_b[:], offs3)
-        nc.sync.dma_start(dy_raw[0][:], dy_rows[:, :, 0:DY_CHUNK])
+        nc.sync.dma_start(dy_first[:], dy_rows[:, :, 0 : 2 * DY_CHUNK])
         nc.sync.dma_start(list_a[:], offs2)
-        for c in range(1, n_chunks):
-            nc.sync.dma_start(dy_raw[c][:], dy_rows[:, :, c * DY_CHUNK : (c + 1) * DY_CHUNK])
+        for c in range(2, n_chunks):
+            nc.sync.dma_start(dy_raw[c], dy_rows[:, :, c * DY_CHUNK : (c + 1) * DY_CHUNK])
         nc.sync.dma_start(ground_sb[:], ground)
         nc.sync.dma_start(old_sb[:], old)
 
@@ -82,9 +84,8 @@ def tile_attend_cpageratio_kernel(tc, tab_words, tab_scales, w1, gain, ground, w
         wo_g = sb.tile([P, R, PACK], BF16, name="wo_g", align_bytes=64)
         w1_codes = sb.tile([P, R], U32, name="w1_codes", align_bytes=64)
         w1_sc = sb.tile([P, R], U8, name="w1_sc", align_bytes=64)
-        wo_codes = sb.tile([P, R], U32, name="wo_codes", align_bytes=64)
         wo_sc = sb.tile([P, R], U8, name="wo_sc", align_bytes=64)
-        nc.scalar.copy(*woven(w1_g, w1_raw))
+        nc.scalar.copy(*woven(w1_g, w1_raw[:]))
 
         tab_sc = sb.tile([P, J], U8, name="tab_sc", align_bytes=64)
         nc.vector.tensor_copy(tab_sc[:], bytes_all[:].indirect(list_tab[:]))
@@ -95,7 +96,7 @@ def tile_attend_cpageratio_kernel(tc, tab_words, tab_scales, w1, gain, ground, w
         h0 = sb.tile([P, J], F32, name="h0")
         halves = [slice(h * JH, (h + 1) * JH) for h in range(2)]
         cols = [slice(h * JH // 16, (h + 1) * JH // 16) for h in range(2)]
-        a_ps = [ps.tile([P, JH], F32, name="a_ps%d" % h) for h in range(2)]
+        a_ps = [ps.tile([P, JH], F32, name="a_ps%d" % h, tag="bank%d" % h) for h in range(2)]
         for h in range(2):
             tab_w = sb.tile([P, JH], U16, name="tab_w%d" % h, align_bytes=64)
             nc.vector.tensor_copy(tab_w[:], words[:].indirect(list_tab[:, cols[h]]))
@@ -106,8 +107,7 @@ def tile_attend_cpageratio_kernel(tc, tab_words, tab_scales, w1, gain, ground, w
         dy_g = [sb.tile([P, DY_CHUNK, PACK], BF16, name="dy_g%d" % c, align_bytes=64) for c in range(n_chunks)]
         dy_sc = sb.tile([P, U], U8, name="dy_sc", align_bytes=64)
 
-        nc.vector.tensor_copy(*woven(wo_g, wo_raw))
-        nc.vector.quantize_mx(wo_codes[:].bitcast(FP8X4), wo_sc[:], wo_g[:].rearrange("p c t -> p (c t)"))
+        nc.vector.tensor_copy(*woven(wo_g, wo_raw[:]))
         for h in range(2):
             nc.vector.tensor_copy(page_b[:].indirect(list_b[:, cols[h]]), a_sb[:, halves[h]])
         for h in range(2):
@@ -120,28 +120,30 @@ def tile_attend_cpageratio_kernel(tc, tab_words, tab_scales, w1, gain, ground, w
         warm_root = sb.tile([P, 1], F32, name="warm_root")
         nc.scalar.activation(warm_root[:], h0[:, J - 1 : J], ACT.Abs_reciprocal_sqrt, bias=1.0, scale=0.0)
         for c in range(1, n_chunks):
-            nc.gpsimd.tensor_scalar(dy_g[c][:], dy_raw[c][:].rearrange("p t c -> p c t"), 1.0, 0.0, ALU.mult, ALU.add)
+            nc.gpsimd.tensor_scalar(dy_g[c][:], dy_raw[c].rearrange("p t c -> p c t"), 1.0, 0.0, ALU.mult, ALU.add)
         nc.vector.tensor_copy(page_a[:].indirect(list_a[:]), h1[:])
         top_t = [ps.tile([P, UH], F32, name="top_t%d" % h) for h in range(2)]
-        top = [ps.tile([P, UH], F32, name="top%d" % h) for h in range(2)]
         top_sb = sb.tile([P, U], F32, name="top_sb")
         blocks = UH // P
         for h in range(2):
             for b in range(blocks):
                 nc.tensor.matmul(top_t[h][:, b * P : (b + 1) * P], lhsT=ground_sb[:, h * UH + b * P : h * UH + (b + 1) * P],
                                  rhs=ident[:], is_transpose=True, start=(b == 0), stop=False)
-        dy_codes = sb.tile([P, U], U32, name="dy_codes", tag="ground_then_codes", align_bytes=64)
+        codes = sb.tile([P, U + R], U32, name="codes", tag="ground_then_codes", align_bytes=64)
+        dy_codes = codes[:, 0:U]
+        wo_codes = codes[:, U : U + R]
+        nc.vector.quantize_mx(wo_codes.bitcast(FP8X4), wo_sc[:], wo_g[:].rearrange("p c t -> p (c t)"))
         for c in range(n_chunks):
             cs = slice(c * DY_CHUNK, (c + 1) * DY_CHUNK)
             nc.vector.quantize_mx(dy_codes[:, cs].bitcast(FP8X4), dy_sc[:, cs], dy_g[c][:].rearrange("p c t -> p (c t)"))
 
         us = [slice(h * UH, (h + 1) * UH) for h in range(2)]
-        c0 = [ps.tile([P, UH], F32, name="c0_%d" % h) for h in range(2)]
+        c0 = [ps.tile([P, UH], F32, name="c0_%d" % h, tag="bank%d" % h) for h in range(2)]
         for h in range(2):
-            nc.tensor.matmul_mx(c0[h][:], lhsT=wo_codes[:].bitcast(FP8X4), lhsT_scale=wo_sc[:],
+            nc.tensor.matmul_mx(c0[h][:], lhsT=wo_codes.bitcast(FP8X4), lhsT_scale=wo_sc[:],
                                 rhs=dy_codes[:, us[h]].bitcast(FP8X4), rhs_scale=dy_sc[:, us[h]], start=True, stop=True)
 
-        sq = dy_raw[0][:].rearrange("p t c -> p (t c)")
+        sq = dy_first[:].rearrange("p t c -> p (t c)")[:, 0:U]
         rs = sb.tile([P, U], F32, name="rs")
         rec = sb.tile([P, U], F32, name="rec")
         for h in range(2):
@@ -160,33 +162,36 @@ def tile_attend_cpageratio_kernel(tc, tab_words, tab_scales, w1, gain, ground, w
             nc.scalar.activation(slope[:, halves[h]], h0_sq[:, halves[h]], ACT.Identity, bias=gain_sb[:, 0:1], scale=neg_gain[:, 0:1])
 
         bend = [
-            dy_raw[n_chunks - 1][:].rearrange("p t c -> p (t c)")[:, 0:UH],
+            sb.tile([P, UH], F32, name="bend0")[:],
             dy_g[n_chunks - 1][:].rearrange("p c t -> p (c t)").bitcast(F32),
         ]
-        for h in range(2):
-            nc.gpsimd.tensor_tensor(bend[h], page_b[:, us[h]], rec[:, us[h]], ALU.mult)
+        nc.vector.tensor_tensor(bend[0], page_b[:, us[0]], rec[:, us[0]], ALU.mult)
+        nc.gpsimd.tensor_tensor(bend[1], page_b[:, us[1]], rec[:, us[1]], ALU.mult)
 
         for h in range(2):
             for b in range(blocks):
                 nc.tensor.matmul(top_t[h][:, b * P : (b + 1) * P], lhsT=page_a[:, h * UH + b * P : h * UH + (b + 1) * P],
                                  rhs=ident[:], is_transpose=True, start=False, stop=(b == blocks - 1))
             nc.scalar.copy(top_sb[:, us[h]], top_t[h][:])
-        for h in range(2):
-            for b in range(UH // P):
-                nc.tensor.transpose(top[h][:, b * P : (b + 1) * P], top_sb[:, h * UH + b * P : h * UH + (b + 1) * P], ident[:])
 
         dpa = sb.tile([P, U], F32, name="dpa")
         dpb = sb.tile([P, U], F32, name="dpb")
-        part = sb.tile([P, U], F32, name="part")
         for h in range(2):
             nc.vector.tensor_tensor(dpa[:, us[h]], c0[h][:], rec[:, us[h]], ALU.mult)
-        dz = sb.tile([P, J], F32, name="dz")
-        nc.vector.tensor_tensor(dz[:], dpa[:].indirect(list_a[:]), slope[:], ALU.mult)
-        rest = sb.tile([P, J], F32, name="rest")
-        nc.gpsimd.tensor_tensor(rest[:], dz[:], old_sb[:], ALU.add)
+        top = [ps.tile([P, UH], F32, name="top%d" % h, tag="bank%d" % h) for h in range(2)]
         for h in range(2):
-            nc.vector.scalar_tensor_tensor(part[:, us[h]], top[h][:], -2.0, bend[h], ALU.mult, ALU.mult)
-        nc.vector.tensor_tensor(dpb[:], part[:], dpa[:], ALU.mult)
+            for b in range(blocks):
+                nc.tensor.transpose(top[h][:, b * P : (b + 1) * P], top_sb[:, h * UH + b * P : h * UH + (b + 1) * P], ident[:])
+        part = [rec[:, us[1]], rec[:, us[0]]]
+        for h in range(2):
+            nc.vector.scalar_tensor_tensor(part[h], dpa[:, us[h]], -2.0, bend[h], ALU.mult, ALU.mult)
+        dz = bend[0]
+        nc.vector.tensor_tensor(dz, dpa[:].indirect(list_a[:]), slope[:], ALU.mult)
+        rest = sb.tile([P, J], F32, name="rest")
+        for h in range(2):
+            nc.gpsimd.tensor_tensor(rest[:, halves[h]], dz[:, halves[h]], old_sb[:, halves[h]], ALU.add)
+        for h in range(2):
+            nc.vector.tensor_tensor(dpb[:, us[h]], top[h][:], part[h], ALU.mult)
         for h in range(2):
             res = sb.tile([P, JH], F32, name="res%d" % h)
             nc.vector.tensor_tensor(res[:], dpb[:].indirect(list_b[:, cols[h]]), rest[:, halves[h]], ALU.add)

@@ -26,7 +26,7 @@ DY_CHUNK = 256
 
 def woven(grouped, raw):
     return (
-        grouped[:].rearrange("p (c i) t -> p c t i", i=4),
+        grouped.rearrange("p (c i t) -> p c t i", i=4, t=PACK),
         raw.rearrange("p t (c i) -> p c t i", i=4),
     )
 
@@ -77,19 +77,19 @@ def tile_attend_cpageratio_kernel(tc, tab_words, tab_scales, w1, gain, ground, w
         nc.sync.dma_start(list_a[:], offs2)
         for c in range(2, n_chunks):
             nc.sync.dma_start(dy_raw[c], dy_rows[:, :, c * DY_CHUNK : (c + 1) * DY_CHUNK])
-        nc.sync.dma_start(ground_sb[:], ground)
         nc.sync.dma_start(old_sb[:], old)
+        nc.sync.dma_start(ground_sb[:], ground)
 
-        w1_g = sb.tile([P, R, PACK], BF16, name="w1_g", align_bytes=64)
-        wo_g = sb.tile([P, R, PACK], BF16, name="wo_g", align_bytes=64)
+        w1_g = sb.tile([P, R * PACK], BF16, name="w1_g", align_bytes=64)
+        wo_g = sb.tile([P, R * PACK], BF16, name="wo_g", align_bytes=64)
         w1_codes = sb.tile([P, R], U32, name="w1_codes", align_bytes=64)
         w1_sc = sb.tile([P, R], U8, name="w1_sc", align_bytes=64)
         wo_sc = sb.tile([P, R], U8, name="wo_sc", align_bytes=64)
-        nc.scalar.copy(*woven(w1_g, w1_raw[:]))
+        nc.scalar.copy(*woven(w1_g[:], w1_raw[:]))
 
         tab_sc = sb.tile([P, J], U8, name="tab_sc", align_bytes=64)
         nc.vector.tensor_copy(tab_sc[:], bytes_all[:].indirect(list_tab[:]))
-        nc.vector.quantize_mx(w1_codes[:].bitcast(FP8X4), w1_sc[:], w1_g[:].rearrange("p c t -> p (c t)"))
+        nc.vector.quantize_mx(w1_codes[:].bitcast(FP8X4), w1_sc[:], w1_g[:])
 
 
         a_sb = sb.tile([P, J], F32, name="a_sb")
@@ -104,10 +104,17 @@ def tile_attend_cpageratio_kernel(tc, tab_words, tab_scales, w1, gain, ground, w
                                 rhs=tab_w[:].bitcast(FP4X4), rhs_scale=tab_sc[:, halves[h]], start=True, stop=True)
             nc.scalar.copy(a_sb[:, halves[h]], a_ps[h][:])
 
-        dy_g = [sb.tile([P, DY_CHUNK, PACK], BF16, name="dy_g%d" % c, align_bytes=64) for c in range(n_chunks)]
+        width = DY_CHUNK * PACK
+        woven_late = sb.tile([P, 2 * width], BF16, name="woven_late", align_bytes=64)
+        dy_g = [
+            sb.tile([P, width], BF16, name="dy_g0", align_bytes=64)[:],
+            sb.tile([P, width], BF16, name="dy_g1", align_bytes=64)[:],
+            woven_late[:, width:],
+            woven_late[:, 0:width],
+        ]
         dy_sc = sb.tile([P, U], U8, name="dy_sc", align_bytes=64)
 
-        nc.vector.tensor_copy(*woven(wo_g, wo_raw[:]))
+        nc.vector.tensor_copy(*woven(wo_g[:], wo_raw[:]))
         for h in range(2):
             nc.vector.tensor_copy(page_b[:].indirect(list_b[:, cols[h]]), a_sb[:, halves[h]])
         for h in range(2):
@@ -120,7 +127,7 @@ def tile_attend_cpageratio_kernel(tc, tab_words, tab_scales, w1, gain, ground, w
         warm_root = sb.tile([P, 1], F32, name="warm_root")
         nc.scalar.activation(warm_root[:], h0[:, J - 1 : J], ACT.Abs_reciprocal_sqrt, bias=1.0, scale=0.0)
         for c in range(1, n_chunks):
-            nc.gpsimd.tensor_scalar(dy_g[c][:], dy_raw[c].rearrange("p t c -> p c t"), 1.0, 0.0, ALU.mult, ALU.add)
+            nc.gpsimd.tensor_scalar(dy_g[c].rearrange("p (c t) -> p c t", t=PACK), dy_raw[c].rearrange("p t c -> p c t"), 1.0, 0.0, ALU.mult, ALU.add)
         nc.vector.tensor_copy(page_a[:].indirect(list_a[:]), h1[:])
         top_t = [ps.tile([P, UH], F32, name="top_t%d" % h) for h in range(2)]
         top_sb = sb.tile([P, U], F32, name="top_sb")
@@ -132,10 +139,10 @@ def tile_attend_cpageratio_kernel(tc, tab_words, tab_scales, w1, gain, ground, w
         codes = sb.tile([P, U + R], U32, name="codes", tag="ground_then_codes", align_bytes=64)
         dy_codes = codes[:, 0:U]
         wo_codes = codes[:, U : U + R]
-        nc.vector.quantize_mx(wo_codes.bitcast(FP8X4), wo_sc[:], wo_g[:].rearrange("p c t -> p (c t)"))
+        nc.vector.quantize_mx(wo_codes.bitcast(FP8X4), wo_sc[:], wo_g[:])
         for c in range(n_chunks):
             cs = slice(c * DY_CHUNK, (c + 1) * DY_CHUNK)
-            nc.vector.quantize_mx(dy_codes[:, cs].bitcast(FP8X4), dy_sc[:, cs], dy_g[c][:].rearrange("p c t -> p (c t)"))
+            nc.vector.quantize_mx(dy_codes[:, cs].bitcast(FP8X4), dy_sc[:, cs], dy_g[c])
 
         us = [slice(h * UH, (h + 1) * UH) for h in range(2)]
         c0 = [ps.tile([P, UH], F32, name="c0_%d" % h, tag="bank%d" % h) for h in range(2)]
@@ -146,6 +153,7 @@ def tile_attend_cpageratio_kernel(tc, tab_words, tab_scales, w1, gain, ground, w
         sq = dy_first[:].rearrange("p t c -> p (t c)")[:, 0:U]
         rs = sb.tile([P, U], F32, name="rs")
         rec = sb.tile([P, U], F32, name="rec")
+        rec2 = sb.tile([P, UH], F32, name="rec2")
         for h in range(2):
             quarters = [slice(h * UH + e * UH // 2, h * UH + (e + 1) * UH // 2) for e in range(2)]
             for s in quarters:
@@ -154,6 +162,9 @@ def tile_attend_cpageratio_kernel(tc, tab_words, tab_scales, w1, gain, ground, w
                 nc.scalar.activation(rs[:, s], sq[:, s], ACT.Abs_reciprocal_sqrt, bias=1.0)
             for s in quarters:
                 nc.scalar.activation(rec[:, s], rs[:, s], ACT.Square)
+            if h == 0:
+                for s in quarters:
+                    nc.scalar.activation(rec2[:, s], rec[:, s], ACT.Square)
         h0_sq = rs[:, us[1]]
         slope = sb.tile([P, J], F32, name="slope")
         for h in range(2):
@@ -161,12 +172,16 @@ def tile_attend_cpageratio_kernel(tc, tab_words, tab_scales, w1, gain, ground, w
         for h in range(2):
             nc.scalar.activation(slope[:, halves[h]], h0_sq[:, halves[h]], ACT.Identity, bias=gain_sb[:, 0:1], scale=neg_gain[:, 0:1])
 
-        bend = [
-            sb.tile([P, UH], F32, name="bend0")[:],
-            dy_g[n_chunks - 1][:].rearrange("p c t -> p (c t)").bitcast(F32),
+        dpa = sb.tile([P, U], F32, name="dpa")
+        bend_early = sb.tile([P, DY_CHUNK], F32, name="bend_early")
+        bend_late = woven_late[:].bitcast(F32)
+        pieces = [
+            (slice(0, DY_CHUNK), bend_early[:], rec2, c0[0]),
+            (slice(DY_CHUNK, UH), bend_late[:, DY_CHUNK:UH], rec2, c0[0]),
+            (us[1], bend_late[:, us[1]], rec, dpa),
         ]
-        nc.vector.tensor_tensor(bend[0], page_b[:, us[0]], rec[:, us[0]], ALU.mult)
-        nc.gpsimd.tensor_tensor(bend[1], page_b[:, us[1]], rec[:, us[1]], ALU.mult)
+        for s, bend, factor, partner in pieces:
+            nc.gpsimd.tensor_tensor(bend, page_b[:, s], factor[:, s], ALU.mult)
 
         for h in range(2):
             for b in range(blocks):
@@ -174,24 +189,23 @@ def tile_attend_cpageratio_kernel(tc, tab_words, tab_scales, w1, gain, ground, w
                                  rhs=ident[:], is_transpose=True, start=False, stop=(b == blocks - 1))
             nc.scalar.copy(top_sb[:, us[h]], top_t[h][:])
 
-        dpa = sb.tile([P, U], F32, name="dpa")
         dpb = sb.tile([P, U], F32, name="dpb")
         for h in range(2):
             nc.vector.tensor_tensor(dpa[:, us[h]], c0[h][:], rec[:, us[h]], ALU.mult)
+        part = sb.tile([P, U], F32, name="part")
+        for s, bend, factor, partner in pieces:
+            nc.vector.scalar_tensor_tensor(part[:, s], partner[:, s], -2.0, bend, ALU.mult, ALU.mult)
         top = [ps.tile([P, UH], F32, name="top%d" % h, tag="bank%d" % h) for h in range(2)]
         for h in range(2):
             for b in range(blocks):
                 nc.tensor.transpose(top[h][:, b * P : (b + 1) * P], top_sb[:, h * UH + b * P : h * UH + (b + 1) * P], ident[:])
-        part = [rec[:, us[1]], rec[:, us[0]]]
-        for h in range(2):
-            nc.vector.scalar_tensor_tensor(part[h], dpa[:, us[h]], -2.0, bend[h], ALU.mult, ALU.mult)
-        dz = bend[0]
+        dz = rec[:, us[1]]
         nc.vector.tensor_tensor(dz, dpa[:].indirect(list_a[:]), slope[:], ALU.mult)
         rest = sb.tile([P, J], F32, name="rest")
         for h in range(2):
             nc.gpsimd.tensor_tensor(rest[:, halves[h]], dz[:, halves[h]], old_sb[:, halves[h]], ALU.add)
         for h in range(2):
-            nc.vector.tensor_tensor(dpb[:, us[h]], top[h][:], part[h], ALU.mult)
+            nc.vector.tensor_tensor(dpb[:, us[h]], top[h][:], part[:, us[h]], ALU.mult)
         for h in range(2):
             res = sb.tile([P, JH], F32, name="res%d" % h)
             nc.vector.tensor_tensor(res[:], dpb[:].indirect(list_b[:, cols[h]]), rest[:, halves[h]], ALU.add)

from contextlib import ExitStack

import concourse.mybir as mybir
from concourse.masks import make_identity

K, R, F, T, J, U = 512, 128, 512, 2048, 512, 1024
FLOPS = 2 * K * R * J + 2 * F * R * U

F32 = mybir.dt.float32
BF16 = mybir.dt.bfloat16
I32 = mybir.dt.int32
U32 = mybir.dt.uint32
U16 = mybir.dt.uint16
U8 = mybir.dt.uint8
FP8X4 = mybir.dt.float8_e4m3fn_x4
FP4X4 = mybir.dt.float4_e2m1fn_x4
ACT = mybir.ActivationFunctionType
ALU = mybir.AluOpType

P = 128
PACK = 4
JH = J // 2
UH = U // 2
DY_CHUNK = 256


def woven(grouped, raw):
    return (
        grouped.rearrange("p (c i t) -> p c t i", i=4, t=PACK),
        raw.rearrange("p t (c i) -> p c t i", i=4),
    )


def tile_attend_cpageratio_kernel(tc, tab_words, tab_scales, w1, gain, ground, wo, dy, old, offs, offs2, offs3, out):
    nc = tc.nc
    with ExitStack() as ctx:
        sb = ctx.enter_context(tc.tile_pool(name="sb", bufs=1))
        ps = ctx.enter_context(tc.psum_pool(name="ps", bufs=1))

        list_tab = sb.tile([P, J // 16], U16, name="list_tab")
        list_a = sb.tile([P, J // 16], U16, name="list_a")
        list_b = sb.tile([P, J // 16], U16, name="list_b")
        words = sb.tile([P, T], U16, name="words")
        bytes_all = sb.tile([P, T], U8, name="bytes_all")
        w1_raw = sb.tile([P, PACK, R], F32, name="w1_raw")
        wo_raw = sb.tile([P, PACK, R], F32, name="wo_raw")
        n_chunks = U // DY_CHUNK
        dy_first = sb.tile([P, PACK, 2 * DY_CHUNK], F32, name="dy_first")
        dy_late = [sb.tile([P, PACK, DY_CHUNK], F32, name="dy_late%d" % c) for c in range(2)]
        dy_raw = [dy_first[:, :, 0:DY_CHUNK], dy_first[:, :, DY_CHUNK : 2 * DY_CHUNK], dy_late[0][:], dy_late[1][:]]
        gain_sb = sb.tile([P, 1], F32, name="gain_sb")
        ground_sb = sb.tile([P, U], F32, name="ground_sb", tag="ground_then_codes", align_bytes=64)
        old_sb = sb.tile([P, J], F32, name="old_sb")
        page_a = sb.tile([P, U], F32, name="page_a")
        page_b = sb.tile([P, U], F32, name="page_b")
        warm = sb.tile([P, 1], F32, name="warm")
        warm_out = sb.tile([P, 1], F32, name="warm_out")

        nc.vector.memset(bytes_all[:].bitcast(I32), 0)
        nc.vector.memset(warm[:], 0.0)
        nc.scalar.activation(warm_out[:], warm[:], ACT.Tanh)
        nc.vector.memset(page_b[:], 0.0)
        nc.vector.memset(page_a[:], 0.0)

        ident = sb.tile([P, P], F32, name="ident")
        make_identity(nc, ident[:])
        dy_rows = dy.rearrange("(p t) u -> p t u", t=PACK)
        nc.sync.dma_start(list_tab[:], offs)
        nc.sync.dma_start(w1_raw[:], w1.rearrange("(p t) r -> p t r", t=PACK))
        for q in range(4):
            nc.sync.dma_start(bytes_all[32 * q : 32 * q + 4, :].bitcast(I32), tab_scales[0, 4 * q : 4 * q + 4, :].bitcast(I32))
        nc.sync.dma_start(words[:].bitcast(I32), tab_words[0].bitcast(I32))
        nc.sync.dma_start(wo_raw[:], wo.rearrange("(p t) r -> p t r", t=PACK))
        nc.sync.dma_start(gain_sb[:], gain)
        nc.sync.dma_start(list_b[:], offs3)
        nc.sync.dma_start(dy_first[:], dy_rows[:, :, 0 : 2 * DY_CHUNK])
        nc.sync.dma_start(list_a[:], offs2)
        for c in range(2, n_chunks):
            nc.sync.dma_start(dy_raw[c], dy_rows[:, :, c * DY_CHUNK : (c + 1) * DY_CHUNK])
        nc.sync.dma_start(old_sb[:], old)
        nc.sync.dma_start(ground_sb[:], ground)

        w1_g = sb.tile([P, R * PACK], BF16, name="w1_g", align_bytes=64)
        wo_g = sb.tile([P, R * PACK], BF16, name="wo_g", align_bytes=64)
        w1_codes = sb.tile([P, R], U32, name="w1_codes", align_bytes=64)
        w1_sc = sb.tile([P, R], U8, name="w1_sc", align_bytes=64)
        wo_sc = sb.tile([P, R], U8, name="wo_sc", align_bytes=64)
        nc.scalar.copy(*woven(w1_g[:], w1_raw[:]))

        tab_sc = sb.tile([P, J], U8, name="tab_sc", align_bytes=64)
        nc.vector.tensor_copy(tab_sc[:], bytes_all[:].indirect(list_tab[:]))
        nc.vector.quantize_mx(w1_codes[:].bitcast(FP8X4), w1_sc[:], w1_g[:])


        a_sb = sb.tile([P, J], F32, name="a_sb")
        h0 = sb.tile([P, J], F32, name="h0")
        halves = [slice(h * JH, (h + 1) * JH) for h in range(2)]
        cols = [slice(h * JH // 16, (h + 1) * JH // 16) for h in range(2)]
        a_ps = [ps.tile([P, JH], F32, name="a_ps%d" % h, tag="bank%d" % h) for h in range(2)]
        for h in range(2):
            tab_w = sb.tile([P, JH], U16, name="tab_w%d" % h, align_bytes=64)
            nc.vector.tensor_copy(tab_w[:], words[:].indirect(list_tab[:, cols[h]]))
            nc.tensor.matmul_mx(a_ps[h][:], lhsT=w1_codes[:].bitcast(FP8X4), lhsT_scale=w1_sc[:],
                                rhs=tab_w[:].bitcast(FP4X4), rhs_scale=tab_sc[:, halves[h]], start=True, stop=True)
            nc.scalar.copy(a_sb[:, halves[h]], a_ps[h][:])

        width = DY_CHUNK * PACK
        woven_late = sb.tile([P, 2 * width], BF16, name="woven_late", align_bytes=64)
        dy_g = [
            sb.tile([P, width], BF16, name="dy_g0", align_bytes=64)[:],
            sb.tile([P, width], BF16, name="dy_g1", align_bytes=64)[:],
            woven_late[:, width:],
            woven_late[:, 0:width],
        ]
        dy_sc = sb.tile([P, U], U8, name="dy_sc", align_bytes=64)

        nc.vector.tensor_copy(*woven(wo_g[:], wo_raw[:]))
        for h in range(2):
            nc.vector.tensor_copy(page_b[:].indirect(list_b[:, cols[h]]), a_sb[:, halves[h]])
        for h in range(2):
            nc.scalar.activation(h0[:, halves[h]], a_ps[h][:], ACT.Tanh)
        neg_gain = sb.tile([P, 1], F32, name="neg_gain")
        nc.gpsimd.tensor_scalar(neg_gain[:], gain_sb[:], -1.0, 0.0, ALU.mult, ALU.add)
        h1 = sb.tile([P, J], F32, name="h1")
        nc.gpsimd.tensor_scalar(h1[:], h0[:], gain_sb[:, 0:1], 1.0, ALU.mult, ALU.mult)
        nc.scalar.copy(*woven(dy_g[0], dy_raw[0]))
        warm_root = sb.tile([P, 1], F32, name="warm_root")
        nc.scalar.activation(warm_root[:], h0[:, J - 1 : J], ACT.Abs_reciprocal_sqrt, bias=1.0, scale=0.0)
        for c in range(1, n_chunks):
            nc.gpsimd.tensor_scalar(dy_g[c].rearrange("p (c t) -> p c t", t=PACK), dy_raw[c].rearrange("p t c -> p c t"), 1.0, 0.0, ALU.mult, ALU.add)
        nc.vector.tensor_copy(page_a[:].indirect(list_a[:]), h1[:])
        top_t = [ps.tile([P, UH], F32, name="top_t%d" % h) for h in range(2)]
        top_sb = sb.tile([P, U], F32, name="top_sb")
        blocks = UH // P
        for h in range(2):
            for b in range(blocks):
                nc.tensor.matmul(top_t[h][:, b * P : (b + 1) * P], lhsT=ground_sb[:, h * UH + b * P : h * UH + (b + 1) * P],
                                 rhs=ident[:], is_transpose=True, start=(b == 0), stop=False)
        codes = sb.tile([P, U + R], U32, name="codes", tag="ground_then_codes", align_bytes=64)
        dy_codes = codes[:, 0:U]
        wo_codes = codes[:, U : U + R]
        nc.vector.quantize_mx(wo_codes.bitcast(FP8X4), wo_sc[:], wo_g[:])
        for c in range(n_chunks):
            cs = slice(c * DY_CHUNK, (c + 1) * DY_CHUNK)
            nc.vector.quantize_mx(dy_codes[:, cs].bitcast(FP8X4), dy_sc[:, cs], dy_g[c])

        us = [slice(h * UH, (h + 1) * UH) for h in range(2)]
        c0 = [ps.tile([P, UH], F32, name="c0_%d" % h, tag="bank%d" % h) for h in range(2)]
        for h in range(2):
            nc.tensor.matmul_mx(c0[h][:], lhsT=wo_codes.bitcast(FP8X4), lhsT_scale=wo_sc[:],
                                rhs=dy_codes[:, us[h]].bitcast(FP8X4), rhs_scale=dy_sc[:, us[h]], start=True, stop=True)

        sq = dy_first[:].rearrange("p t c -> p (t c)")[:, 0:U]
        rs = sb.tile([P, U], F32, name="rs")
        rec = sb.tile([P, U], F32, name="rec")
        rec2 = sb.tile([P, UH], F32, name="rec2")
        for h in range(2):
            quarters = [slice(h * UH + e * UH // 2, h * UH + (e + 1) * UH // 2) for e in range(2)]
            for s in quarters:
                nc.scalar.activation(sq[:, s], page_b[:, s], ACT.Square)
            for s in quarters:
                nc.scalar.activation(rs[:, s], sq[:, s], ACT.Abs_reciprocal_sqrt, bias=1.0)
            for s in quarters:
                nc.scalar.activation(rec[:, s], rs[:, s], ACT.Square)
            if h == 0:
                for s in quarters:
                    nc.scalar.activation(rec2[:, s], rec[:, s], ACT.Square)
        h0_sq = rs[:, us[1]]
        slope = sb.tile([P, J], F32, name="slope")
        for h in range(2):
            nc.scalar.activation(h0_sq[:, halves[h]], h0[:, halves[h]], ACT.Square)
        for h in range(2):
            nc.scalar.activation(slope[:, halves[h]], h0_sq[:, halves[h]], ACT.Identity, bias=gain_sb[:, 0:1], scale=neg_gain[:, 0:1])

        dpa = sb.tile([P, U], F32, name="dpa")
        bend_early = sb.tile([P, DY_CHUNK], F32, name="bend_early")
        bend_late = woven_late[:].bitcast(F32)
        pieces = [
            (slice(0, DY_CHUNK), bend_early[:], rec2, c0[0]),
            (slice(DY_CHUNK, UH), bend_late[:, DY_CHUNK:UH], rec2, c0[0]),
            (us[1], bend_late[:, us[1]], rec, dpa),
        ]
        for s, bend, factor, partner in pieces:
            nc.gpsimd.tensor_tensor(bend, page_b[:, s], factor[:, s], ALU.mult)

        for h in range(2):
            for b in range(blocks):
                nc.tensor.matmul(top_t[h][:, b * P : (b + 1) * P], lhsT=page_a[:, h * UH + b * P : h * UH + (b + 1) * P],
                                 rhs=ident[:], is_transpose=True, start=False, stop=(b == blocks - 1))
            nc.scalar.copy(top_sb[:, us[h]], top_t[h][:])

        dpb = sb.tile([P, U], F32, name="dpb")
        for h in range(2):
            nc.vector.tensor_tensor(dpa[:, us[h]], c0[h][:], rec[:, us[h]], ALU.mult)
        part = sb.tile([P, U], F32, name="part")
        for s, bend, factor, partner in pieces:
            nc.vector.scalar_tensor_tensor(part[:, s], partner[:, s], -2.0, bend, ALU.mult, ALU.mult)
        top = [ps.tile([P, UH], F32, name="top%d" % h, tag="bank%d" % h) for h in range(2)]
        for h in range(2):
            for b in range(blocks):
                nc.tensor.transpose(top[h][:, b * P : (b + 1) * P], top_sb[:, h * UH + b * P : h * UH + (b + 1) * P], ident[:])
        dz = rec[:, us[1]]
        nc.vector.tensor_tensor(dz, dpa[:].indirect(list_a[:]), slope[:], ALU.mult)
        rest = sb.tile([P, J], F32, name="rest")
        for h in range(2):
            nc.gpsimd.tensor_tensor(rest[:, halves[h]], dz[:, halves[h]], old_sb[:, halves[h]], ALU.add)
        for h in range(2):
            nc.vector.tensor_tensor(dpb[:, us[h]], top[h][:], part[:, us[h]], ALU.mult)
        for h in range(2):
            res = sb.tile([P, JH], F32, name="res%d" % h)
            nc.vector.tensor_tensor(res[:], dpb[:].indirect(list_b[:, cols[h]]), rest[:, halves[h]], ALU.add)
            nc.sync.dma_start(out[:, halves[h]], res[:])
